import numpy as np
import ml_dtypes


def mxq(x, axis, fmt="e4m3"):
    dtype, down = {"e4m3": (ml_dtypes.float8_e4m3fn, 7), "e5m2": (ml_dtypes.float8_e5m2, 14)}[fmt]
    v = np.moveaxis(np.asarray(x, np.float32).astype(ml_dtypes.bfloat16).astype(np.float64), axis, -1)
    blocks = v.reshape(v.shape[:-1] + (-1, 32))
    amax = np.abs(blocks).max(-1, keepdims=True)
    byte = np.maximum(np.where(amax > 0, np.frexp(amax)[1] - 1 + 127, 0) - down, 1)
    scale = np.exp2(byte - 127.0)
    codes = (blocks / scale).astype(np.float32).astype(dtype).astype(np.float64)
    return np.moveaxis((codes * scale).reshape(v.shape), -1, axis)


WIDE = False


def mx_kscale(k):
    if not WIDE:
        return np.ones(k)
    levels = np.array([10, -10, 5, -5, 0])
    if k % 512:
        return np.exp2(np.random.permutation(np.resize(levels, k // 32))).repeat(32)
    a = np.empty((k // 512, 16))
    for p in range(k // 512):
        a[p, :8] = np.random.permutation(np.resize(levels, 8))
        for g in range(8):
            far = levels[np.abs(levels - a[p, g]) >= 10]
            a[p, g + 8] = far[np.random.randint(len(far))]
    return np.exp2(a.ravel()).repeat(32)


def f64(x):
    return np.asarray(x).astype(np.float64)


def striped(idx):
    return np.tile(idx.reshape(-1, 16).T, (8, 1)).astype(np.uint16)


def unstriped(offs):
    return offs[:16].T.reshape(-1).astype(np.int64)


def striped8(idx):
    return np.concatenate([x.reshape(-1, 16).T for x in idx]).astype(np.uint16)


def runs(offs, k):
    lists = np.stack([offs[16 * r : 16 * r + 16].T.reshape(-1) for r in range(8)]).astype(np.int64)
    return lists[np.arange(k) % 512 // 64]


def pack_weight(w):
    k, n = w.shape
    w = f64(np.asarray(w, np.float32).astype(ml_dtypes.bfloat16)).reshape(k // 32, 32, n)
    amax = np.abs(w).max(1)
    byte = np.clip(np.where(amax > 0, np.frexp(amax)[1] - 1 + 127 - 7, 1), 1, 254)
    scaled = (w * np.exp2(127.0 - byte)[:, None, :]).reshape(k, n).astype(np.float32)
    words = np.ascontiguousarray(scaled.reshape(k // 512, 128, 4, n).transpose(0, 1, 3, 2)).astype(ml_dtypes.float8_e4m3fn).view(np.uint8)
    return words, np.ascontiguousarray(byte.astype(np.uint8).reshape(k // 512, 16, n))


def unpack_weight(words, scales):
    g, p, n, _ = words.shape
    vals = np.ascontiguousarray(words).view(ml_dtypes.float8_e4m3fn).astype(np.float64) * np.repeat(np.exp2(scales.astype(np.float64) - 127.0), 8, axis=1)[..., None]
    return vals.transpose(0, 1, 3, 2).reshape(g * 512, n)


E2M1 = np.array([0.0, 0.5, 1.0, 1.5, 2.0, 3.0, 4.0, 6.0, -0.0, -0.5, -1.0, -1.5, -2.0, -3.0, -4.0, -6.0])


def pack_fp4(w):
    k, n = w.shape
    w = f64(np.asarray(w, np.float32).astype(ml_dtypes.bfloat16)).reshape(k // 32, 32, n)
    amax = np.abs(w).max(1)
    mant, ex = np.frexp(amax / 6.0)
    byte = np.clip(np.where(amax > 0, np.where(mant > 0.5, ex, ex - 1) + 127, 1), 1, 254)
    scaled = (w * np.exp2(127.0 - byte)[:, None, :]).reshape(k, n).astype(np.float32)
    c = np.ascontiguousarray(scaled.reshape(k // 512, 128, 4, n).transpose(0, 1, 3, 2)).astype(ml_dtypes.float4_e2m1fn).view(np.uint8) & 0xF
    words = (c[..., 0::2] | (c[..., 1::2] << 4)).reshape(k // 512, 128, 2 * n)
    return np.ascontiguousarray(words), np.ascontiguousarray(byte.astype(np.uint8).reshape(k // 512, 16, n))


def unpack_fp4(words, scales):
    g, _, n = scales.shape
    words = np.ascontiguousarray(words).reshape(g, 128, n, 2)
    nib = np.empty((g, 128, n, 4), np.uint8)
    nib[..., 0::2] = words & 0xF
    nib[..., 1::2] = words >> 4
    vals = E2M1[nib] * np.repeat(np.exp2(scales.astype(np.float64) - 127.0), 8, axis=1)[..., None]
    return vals.transpose(0, 1, 3, 2).reshape(g * 512, n)


def planes(y):
    n, m = y.shape
    v = y.astype(np.float32).astype(ml_dtypes.bfloat16).astype(np.float64).reshape(n // 32, 32, m)
    top = np.abs(v).max(1)
    byte = np.clip(np.where(top > 0, np.frexp(top)[1] - 1 + 127 - 7, 1), 1, 254)
    codes = (v * np.exp2(127.0 - byte)[:, None, :]).reshape(n, m).astype(np.float32).astype(ml_dtypes.float8_e4m3fn).view(np.uint8)
    words = codes.reshape(n // 512, 128, 4, m).transpose(0, 1, 3, 2)
    return np.ascontiguousarray(words), np.ascontiguousarray(byte.astype(np.uint8).reshape(n // 512, 16, m))


K, T, S, V, H, U = 512, 2048, 512, 512, 512, 1024


def setup_inputs():
    n = np.random.standard_normal
    s = mx_kscale(K)[:, None]
    u = mx_kscale(S)
    packed_xT = pack_weight(n((K, T)) * s)
    packed_w1 = pack_fp4(n((K, H)) / np.sqrt(K) / s)
    packed_w2 = pack_fp4(n((K, H)) / np.sqrt(K) / s)
    return {
        "x_words": packed_xT[0],
        "x_scales": packed_xT[1],
        "w1_words": packed_w1[0],
        "w1_scales": packed_w1[1],
        "w2_words": packed_w2[0],
        "w2_scales": packed_w2[1],
        "ga": (np.random.uniform(0.5, 1.5, (H, 1)) * u[:, None]).astype(np.float32),
        "gb": (np.random.uniform(0.5, 1.5, (H, 1)) / u[:, None]).astype(np.float32),
        "mem": n((S, U)).astype(np.float32),
        "offs": striped8(np.random.randint(0, T, (8, S))),
        "two": striped(np.random.permutation(T)[:V]),
        "n1": striped8(np.stack([np.random.permutation(S) for _ in range(8)])),
        "n2": striped8(np.stack([np.random.permutation(S) for _ in range(8)])),
        "n3": striped8(np.stack([np.random.permutation(V) for _ in range(8)])),
        "n4": striped8(np.stack([np.random.permutation(V) for _ in range(8)])),
        "n5": striped8(np.stack([np.random.permutation(U)[:V] for _ in range(8)])),
    }


def reference(x_words, x_scales, w1_words, w1_scales, w2_words, w2_scales, ga, gb, mem, offs, two, n1, n2, n3, n4, n5):
    xq = unpack_weight(x_words, x_scales)[np.arange(K)[:, None], runs(offs, K)]
    a = unpack_fp4(w1_words, w1_scales).T @ xq
    pa = a[np.arange(H)[:, None], runs(n1, H)]
    pb = a[np.arange(H)[:, None], runs(n2, H)]
    z = f64(ga) * (np.maximum(np.minimum(a, pa), np.minimum(np.maximum(a, pa), pb)))
    x_two = unpack_weight(x_words, x_scales)[:, unstriped(two)]
    b = unpack_fp4(w2_words, w2_scales).T @ x_two
    ex = np.exp(0.5 * b)
    z2 = f64(gb) * ((2.0 * ex) / (ex + ex[np.arange(H)[:, None], runs(n3, H)] + ex[np.arange(H)[:, None], runs(n4, H)]))
    s = 0.0625 * ((mxq(z, 0, "e4m3").T @ mxq(z2, 0, "e4m3")))
    nw = np.maximum(s, 0.5 * (f64(mem)[np.arange(S)[:, None], runs(n5, S)]))
    out = f64(mem).copy()
    out[np.arange(S)[:, None], runs(n5, S)] = nw
    return (out,) + planes(out)

@@ -1,0 +1,285 @@
+from contextlib import ExitStack
+
+import concourse.mybir as mybir
+from concourse.masks import make_identity
+
+K, T, S, V, H, U = 512, 2048, 512, 512, 512, 1024
+P = 128
+SLOTS = 4
+FLOPS = 3 * 2 * 512 * 512 * 512
+
+F32 = mybir.dt.float32
+BF16 = mybir.dt.bfloat16
+I32 = mybir.dt.int32
+U32 = mybir.dt.uint32
+U16 = mybir.dt.uint16
+U8 = mybir.dt.uint8
+FP8X4 = mybir.dt.float8_e4m3fn_x4
+FP4X4 = mybir.dt.float4_e2m1fn_x4
+ALU = mybir.AluOpType
+ACT = mybir.ActivationFunctionType
+
+CHUNKS = 2
+VC = V // CHUNKS
+QUARTERS = 4
+UQ = U // QUARTERS
+
+
+def tile_picked_hkqmedsharepagex_none_po_kernel(
+    tc, x_words, x_scales, w1_words, w1_scales, w2_words, w2_scales, ga, gb, mem,
+    offs, two, n1, n2, n3, n4, n5, out_0, out_1, out_2,
+):
+    nc = tc.nc
+    with ExitStack() as ctx:
+        lists = ctx.enter_context(tc.tile_pool(name="lists", bufs=1))
+        sb = ctx.enter_context(tc.tile_pool(name="sb", bufs=1))
+        early = ctx.enter_context(tc.tile_pool(name="early", bufs=1))
+        psum = ctx.enter_context(tc.psum_pool(name="psum", bufs=1))
+
+        def tile(name, shape, dtype):
+            return sb.tile(shape, dtype, name=name, align_bytes=64)
+
+        def bank(i, name, shape):
+            return psum.tile(shape, F32, name=name, tag="bank%d" % i)
+
+        def load_list(name, src):
+            t = lists.tile([P, 32], U16, name=name)
+            nc.sync.dma_start(t[:], src)
+            return t
+
+        def gather(on_scalar, out, window, offsets):
+            if on_scalar:
+                nc.scalar.activation(out, window.indirect(offsets), ACT.Copy)
+            else:
+                nc.vector.tensor_copy(out, window.indirect(offsets))
+
+        xs = early.tile([P, T], U8, name="xs", align_bytes=64, offset=16384)
+        nc.gpsimd.memset(xs[:].bitcast(I32), 0)
+        nc.scalar.dma_start(xs[0:P:8, :].bitcast(I32), x_scales[0].bitcast(I32))
+        offs_t = load_list("offs_t", offs)
+        two_t = load_list("two_t", two)
+        ws_raw = tile("ws_raw", [16, 2 * H], U8)
+        for i, src in enumerate((w1_scales, w2_scales)):
+            nc.sync.dma_start(ws_raw[:, i * H : (i + 1) * H].bitcast(I32), src[0].bitcast(I32))
+        xw = early.tile([P, T], I32, name="xw", align_bytes=64, offset=8192)
+        nc.sync.dma_start(xw[:], x_words[0].rearrange("p n t -> p (n t)").bitcast(I32))
+        w_raw = [early.tile([P, 2 * H], U8, name="w_raw%d" % i, align_bytes=64, offset=1024 * i) for i in range(2)]
+        for i, words in enumerate((w1_words, w2_words)):
+            nc.sync.dma_start(w_raw[i][:].bitcast(I32), words[0].bitcast(I32))
+        n1_t = load_list("n1_t", n1)
+        n2_t = load_list("n2_t", n2)
+        n3_t = load_list("n3_t", n3)
+        n4_t = load_list("n4_t", n4)
+        n5_t = load_list("n5_t", n5)
+
+        g_rows = tile("g_rows", [P, P], F32)
+        nc.vector.memset(g_rows[:], 0.0)
+        for i, factor in enumerate((ga, gb)):
+            nc.gpsimd.dma_start(
+                g_rows[SLOTS * i : SLOTS * (i + 1), :].rearrange("t (b q) -> t b q", q=8),
+                factor.rearrange("(b t q) o -> t b (q o)", t=SLOTS, q=8),
+            )
+        ws = tile("ws", [P, 2 * H], U8)
+        nc.vector.memset(ws[:].bitcast(I32), 0)
+        xsc = tile("xsc", [P, 2 * S], U8)
+        nc.vector.memset(xsc[:].bitcast(I32), 0)
+        ident = tile("ident", [P, P], F32)
+        make_identity(nc, ident[:])
+        a_win = [tile("a_win%d" % t, [P, 2 * S], F32) for t in range(SLOTS)]
+        for t in range(SLOTS):
+            nc.vector.memset(a_win[t][:, S:], 0.0)
+
+        nc.vector.tensor_copy(
+            ws[0:16, :].bitcast(I32).rearrange("p (i t b w) -> p i t b w", i=2, t=SLOTS, w=2),
+            ws_raw[:].bitcast(I32).rearrange("p (i b t w) -> p i t b w", i=2, t=SLOTS, w=2),
+        )
+        for q in range(1, 4):
+            nc.scalar.dma_start(ws[32 * q : 32 * q + 4, :].bitcast(I32), ws[4 * q : 4 * q + 4, :].bitcast(I32))
+        w_dealt = [tile("w_dealt%d" % i, [P, 2 * H], U8) for i in range(2)]
+        for i in range(2):
+            nc.gpsimd.tensor_copy(
+                w_dealt[i][:].bitcast(I32).rearrange("p (t b w) -> p t b w", t=SLOTS, w=4),
+                w_raw[i][:].bitcast(I32).rearrange("p (b t w) -> p t b w", t=SLOTS, w=4),
+            )
+
+        gs = early.tile([P, 2 * S], U8, name="gs", align_bytes=64, offset=4096)
+        for i, lst in enumerate((offs_t, two_t)):
+            nc.vector.tensor_copy(gs[:, i * S : (i + 1) * S], xs[:].indirect(lst[:]))
+        for r in range(4):
+            nc.scalar.dma_start(xsc[r:P:32, :].bitcast(I32), gs[8 * r : P : 32, :].bitcast(I32))
+        gw = [early.tile([P, S], U32, name="gw%d" % i, align_bytes=64, offset=16384 + 1024 * i + 1024 * i) for i in range(2)]
+        for i, lst in enumerate((offs_t, two_t)):
+            nc.vector.tensor_copy(gw[i][:], xw[:].bitcast(U32).indirect(lst[:]))
+
+        g_ps = bank(7, "g_ps", [P, P])
+        nc.tensor.transpose(g_ps[:], g_rows[:], ident[:])
+        ga_c = tile("ga_c", [P, SLOTS], F32)
+        gb2_c = tile("gb2_c", [P, SLOTS], F32)
+        nc.vector.tensor_copy(ga_c[:], g_ps[:, 0:SLOTS])
+        nc.vector.tensor_scalar(gb2_c[:], g_ps[:, SLOTS : 2 * SLOTS], 2.0, None, ALU.mult)
+
+        def first_product(i, t, name):
+            acc = bank(SLOTS * i + t, name, [P, S])
+            nc.tensor.matmul_mx(
+                acc[:],
+                lhsT=w_dealt[i][:, 2 * P * t : 2 * P * (t + 1)].bitcast(FP4X4),
+                lhsT_scale=ws[:, i * H + P * t : i * H + P * (t + 1)],
+                rhs=gw[i][:].bitcast(FP8X4),
+                rhs_scale=xsc[:, i * S : (i + 1) * S],
+                start=True, stop=True,
+            )
+            return acc
+
+        ex = [tile("ex%d" % t, [P, V], F32) for t in range(SLOTS)]
+        a_bf = tile("a_bf", [P, SLOTS, S], BF16)
+        for t in range(SLOTS):
+            a_ps = first_product(0, t, "a_ps%d" % t)
+            nc.vector.tensor_scalar(a_win[t][:, :S], a_ps[:], ga_c[:, t : t + 1], None, ALU.mult)
+            b_ps = first_product(1, t, "b_ps%d" % t)
+            nc.scalar.activation(ex[t][:], b_ps[:], ACT.Exp, scale=0.5)
+
+        page = [early.tile([P, U], F32, name="page%d" % t, align_bytes=64, offset=4096 * t) for t in range(SLOTS)]
+        mem_v = mem.rearrange("(p t) u -> p t u", t=SLOTS)
+        out_v = out_0.rearrange("(p t) u -> p t u", t=SLOTS)
+        for t in range(SLOTS):
+            nc.sync.dma_start(page[t][:], mem_v[:, t, :])
+
+        pa = tile("pa", [P, SLOTS, S], BF16)
+        pb = tile("pb", [P, SLOTS, S], BF16)
+        lo = tile("lo", [P, SLOTS, S], BF16)
+        hi = tile("hi", [P, SLOTS, S], BF16)
+        mid = tile("mid", [P, SLOTS, S], BF16)
+        z_pl = tile("z_pl", [P, SLOTS, S], BF16)
+        for h in range(2):
+            pair = slice(2 * h, 2 * h + 2)
+            for t in (2 * h, 2 * h + 1):
+                gather(False, pa[:, t, :], a_win[t][:], n1_t[:])
+                gather(h == 0, pb[:, t, :], a_win[t][:], n2_t[:])
+                nc.vector.tensor_copy(a_bf[:, t, :], a_win[t][:, :S])
+            nc.vector.tensor_tensor(hi[:, pair, :], a_bf[:, pair, :], pa[:, pair, :], ALU.max)
+            nc.vector.tensor_tensor(lo[:, pair, :], a_bf[:, pair, :], pa[:, pair, :], ALU.min)
+            nc.vector.tensor_tensor(mid[:, pair, :], hi[:, pair, :], pb[:, pair, :], ALU.min)
+            nc.vector.tensor_tensor(z_pl[:, pair, :], lo[:, pair, :], mid[:, pair, :], ALU.max)
+        z_il = tile("z_il", [P, SLOTS * S], BF16)
+        nc.vector.tensor_copy(
+            z_il[:].rearrange("p (t a i s) -> p a t i s", t=SLOTS, i=2, s=SLOTS),
+            z_pl[:].rearrange("p s (a i t) -> p a t i s", t=SLOTS, i=2),
+        )
+        zq = tile("zq", [P, S], U32)
+        zs = tile("zs", [P, S], U8)
+        nc.vector.quantize_mx(zq[:].bitcast(FP8X4), zs[:], z_il[:])
+
+        def denominators(c):
+            cols = slice(c * VC // 16, (c + 1) * VC // 16)
+            g3 = tile("g3_%d" % c, [P, SLOTS, VC], F32)
+            g4 = tile("g4_%d" % c, [P, SLOTS, VC], F32)
+            for t in range(SLOTS):
+                gather(True, g3[:, t, :], ex[t][:], n3_t[:, cols])
+                gather(True, g4[:, t, :], ex[t][:], n4_t[:, cols])
+            r_t = []
+            for vb in range(2):
+                den = bank(4 * c + vb, "den%d_%d" % (c, vb), [P, SLOTS, P])
+                for t in range(SLOTS):
+                    blk = slice(vb * P, (vb + 1) * P)
+                    terms = (ex[t][:, c * VC + vb * P : c * VC + (vb + 1) * P], g3[:, t, blk], g4[:, t, blk])
+                    for n, term in enumerate(terms):
+                        nc.tensor.matmul(den[:, t, :], term, ident[:], start=(n == 0), stop=(n == 2), is_transpose=True)
+                rt = tile("rt%d_%d" % (c, vb), [P, SLOTS, P], F32)
+                nc.scalar.activation(rt[:], den[:], ACT.Abs_reciprocal_sqrt)
+                rt2 = tile("rt2_%d_%d" % (c, vb), [P, SLOTS, P], F32)
+                nc.scalar.activation(rt2[:], rt[:], ACT.Square)
+                r_t.append(rt2)
+            r_ps = []
+            for h in range(2):
+                r = bank(4 + 2 * c + h, "r%d_%d" % (c, h), [P, 2, VC])
+                for tt in range(2):
+                    for vb in range(2):
+                        nc.tensor.transpose(r[:, tt, vb * P : (vb + 1) * P], r_t[vb][:, 2 * h + tt, :], ident[:])
+                r_ps.append(r)
+            return r_ps
+
+        def second_factor(c, r_ps):
+            z2_pl = sb.tile([P, SLOTS, VC], BF16, name="z2_pl%d" % c, tag="z2_pl%d" % c, align_bytes=64)
+            for t in range(SLOTS):
+                nc.vector.scalar_tensor_tensor(
+                    z2_pl[:, t, :], ex[t][:, c * VC : (c + 1) * VC], gb2_c[:, t : t + 1], r_ps[t // 2][:, t % 2, :], ALU.mult, ALU.mult
+                )
+            z2_il = sb.tile([P, VC, SLOTS], BF16, name="z2_il%d" % c, tag="z2_il%d" % c, align_bytes=64)
+            dst = z2_il[:].rearrange("p (a i) s -> p a s i", i=4)
+            src = z2_pl[:].rearrange("p s (a i) -> p a s i", i=4)
+            if c == 0:
+                nc.vector.tensor_copy(dst, src)
+            else:
+                nc.scalar.copy(dst, src)
+            z2q = tile("z2q%d" % c, [P, VC], U32)
+            z2s = tile("z2s%d" % c, [P, VC], U8)
+            nc.vector.quantize_mx(z2q[:].bitcast(FP8X4), z2s[:], z2_il[:].rearrange("p v s -> p (v s)"))
+            return z2q, z2s
+
+        y_pl = tile("y_pl", [P, SLOTS, U], BF16)
+
+        def write_page(c, halves, z2q, z2s):
+            cols = slice(c * VC // 16, (c + 1) * VC // 16)
+            for h in halves:
+                s_ps = bank(2 * c + h, "s%d_%d" % (c, h), [P, 2, VC])
+                for tt in range(2):
+                    t = 2 * h + tt
+                    nc.tensor.matmul_mx(
+                        s_ps[:, tt, :],
+                        lhsT=zq[:, P * t : P * (t + 1)].bitcast(FP8X4),
+                        lhsT_scale=zs[:, P * t : P * (t + 1)],
+                        rhs=z2q[:].bitcast(FP8X4),
+                        rhs_scale=z2s[:],
+                        start=True, stop=True,
+                    )
+                for tt in range(2):
+                    t = 2 * h + tt
+                    tag = {(0, 2): "ex3", (0, 3): "z2_il1"}.get((c, t), "nw%d_%d" % (c, t))
+                    nw = sb.tile([P, VC], F32, name="nw%d_%d" % (c, t), tag=tag, align_bytes=64)
+                    nc.vector.scalar_tensor_tensor(
+                        nw[:], s_ps[:, tt, :], 0.0625, held[:, t, c * VC : (c + 1) * VC], ALU.mult, ALU.max
+                    )
+                    nc.vector.tensor_copy(page[t][:].indirect(n5_t[:, cols]), nw[:])
+                    if c == CHUNKS - 1:
+                        nc.sync.dma_start(out_v[:, t, :], page[t][:])
+                        if t < SLOTS - 1:
+                            nc.scalar.copy(y_pl[:, t, :], page[t][:])
+                        else:
+                            nc.vector.tensor_copy(y_pl[:, t, : U // 2], page[t][:, : U // 2])
+                            nc.scalar.copy(y_pl[:, t, U // 2 :], page[t][:, U // 2 :])
+
+        held = tile("held", [P, SLOTS, V], F32)
+
+        def hold(t):
+            nc.scalar.activation(held[:, t, :], page[t][:].indirect(n5_t[:]), ACT.Copy, scale=0.5)
+
+        z2_0 = second_factor(0, denominators(0))
+        hold(0)
+        hold(1)
+        write_page(0, (0,), *z2_0)
+        hold(2)
+        hold(3)
+        z2_1 = second_factor(1, denominators(1))
+        write_page(0, (1,), *z2_0)
+        write_page(1, (0, 1), *z2_1)
+
+        ys = tile("ys", [P, U], U8)
+        words_v = out_1[0].rearrange("p n t -> p (n t)").bitcast(I32)
+        yq = [tile("yq%d" % h, [P, U // 2], U32) for h in range(2)]
+        for n in range(QUARTERS):
+            cols = slice(n * UQ, (n + 1) * UQ)
+            y_il = tile("y_il%d" % n, [P, UQ, SLOTS], BF16)
+            dst = y_il[:].rearrange("p (a i) s -> p a s i", i=4)
+            src = y_pl[:, :, cols].rearrange("p s (a i) -> p a s i", i=4)
+            if n < 2:
+                nc.vector.tensor_copy(dst, src)
+            else:
+                nc.scalar.copy(dst, src)
+            nc.vector.quantize_mx(
+                yq[n // 2][:, (n % 2) * UQ : (n % 2 + 1) * UQ].bitcast(FP8X4), ys[:, cols], y_il[:].rearrange("p v s -> p (v s)")
+            )
+            if n % 2 == 1:
+                h = n // 2
+                nc.sync.dma_start(words_v[:, h * U // 2 : (h + 1) * U // 2], yq[h][:].bitcast(I32))
+        for q in range(4):
+            nc.sync.dma_start(out_2[0, 4 * q : 4 * q + 4, :].bitcast(I32), ys[32 * q : 32 * q + 4, :].bitcast(I32))

@@ -53,25 +53,26 @@ def tile_picked_hkqmedsharepagex_none_po_kernel(
             else:
                 nc.vector.tensor_copy(out, window.indirect(offsets))
 
-        xs = early.tile([P, T], U8, name="xs", align_bytes=64, offset=16384)
-        nc.gpsimd.memset(xs[:].bitcast(I32), 0)
-        nc.scalar.dma_start(xs[0:P:8, :].bitcast(I32), x_scales[0].bitcast(I32))
+        xs = early.tile([P, T], U8, name="xs", align_bytes=64, offset=17408)
+        nc.vector.memset(xs[:].bitcast(I32), 0)
+        nc.sync.dma_start(xs[0:P:8, :].bitcast(I32), x_scales[0].bitcast(I32))
         offs_t = load_list("offs_t", offs)
         two_t = load_list("two_t", two)
         ws_raw = tile("ws_raw", [16, 2 * H], U8)
         for i, src in enumerate((w1_scales, w2_scales)):
             nc.sync.dma_start(ws_raw[:, i * H : (i + 1) * H].bitcast(I32), src[0].bitcast(I32))
+        w_raw = [early.tile([P, 2 * H], U8, name="w_raw%d" % i, align_bytes=64, offset=1024 * i) for i in range(2)]
+        nc.sync.dma_start(w_raw[0][:].bitcast(I32), w1_words[0].bitcast(I32))
         xw = early.tile([P, T], I32, name="xw", align_bytes=64, offset=8192)
         nc.sync.dma_start(xw[:], x_words[0].rearrange("p n t -> p (n t)").bitcast(I32))
-        w_raw = [early.tile([P, 2 * H], U8, name="w_raw%d" % i, align_bytes=64, offset=1024 * i) for i in range(2)]
-        for i, words in enumerate((w1_words, w2_words)):
-            nc.sync.dma_start(w_raw[i][:].bitcast(I32), words[0].bitcast(I32))
+        nc.sync.dma_start(w_raw[1][:].bitcast(I32), w2_words[0].bitcast(I32))
         n1_t = load_list("n1_t", n1)
         n2_t = load_list("n2_t", n2)
         n3_t = load_list("n3_t", n3)
         n4_t = load_list("n4_t", n4)
         n5_t = load_list("n5_t", n5)
 
+        w_dealt = [tile("w_dealt%d" % i, [P, 2 * H], U8) for i in range(2)]
         g_rows = tile("g_rows", [P, P], F32)
         nc.vector.memset(g_rows[:], 0.0)
         for i, factor in enumerate((ga, gb)):
@@ -85,9 +86,7 @@ def tile_picked_hkqmedsharepagex_none_po_kernel(
         nc.vector.memset(xsc[:].bitcast(I32), 0)
         ident = tile("ident", [P, P], F32)
         make_identity(nc, ident[:])
-        a_win = [tile("a_win%d" % t, [P, 2 * S], F32) for t in range(SLOTS)]
-        for t in range(SLOTS):
-            nc.vector.memset(a_win[t][:, S:], 0.0)
+        a_win = [tile("a_win%d" % t, [P, S], F32) for t in range(SLOTS)]
 
         nc.vector.tensor_copy(
             ws[0:16, :].bitcast(I32).rearrange("p (i t b w) -> p i t b w", i=2, t=SLOTS, w=2),
@@ -95,20 +94,18 @@ def tile_picked_hkqmedsharepagex_none_po_kernel(
         )
         for q in range(1, 4):
             nc.scalar.dma_start(ws[32 * q : 32 * q + 4, :].bitcast(I32), ws[4 * q : 4 * q + 4, :].bitcast(I32))
-        w_dealt = [tile("w_dealt%d" % i, [P, 2 * H], U8) for i in range(2)]
-        for i in range(2):
-            nc.gpsimd.tensor_copy(
-                w_dealt[i][:].bitcast(I32).rearrange("p (t b w) -> p t b w", t=SLOTS, w=4),
-                w_raw[i][:].bitcast(I32).rearrange("p (b t w) -> p t b w", t=SLOTS, w=4),
-            )
 
         gs = early.tile([P, 2 * S], U8, name="gs", align_bytes=64, offset=4096)
         for i, lst in enumerate((offs_t, two_t)):
             nc.vector.tensor_copy(gs[:, i * S : (i + 1) * S], xs[:].indirect(lst[:]))
         for r in range(4):
             nc.scalar.dma_start(xsc[r:P:32, :].bitcast(I32), gs[8 * r : P : 32, :].bitcast(I32))
-        gw = [early.tile([P, S], U32, name="gw%d" % i, align_bytes=64, offset=16384 + 1024 * i + 1024 * i) for i in range(2)]
+        gw = [early.tile([P, S], U32, name="gw%d" % i, align_bytes=64, offset=16384 + 2048 * i) for i in range(2)]
         for i, lst in enumerate((offs_t, two_t)):
+            nc.vector.tensor_copy(
+                w_dealt[i][:].bitcast(I32).rearrange("p (t b w) -> p t b w", t=SLOTS, w=4),
+                w_raw[i][:].bitcast(I32).rearrange("p (b t w) -> p t b w", t=SLOTS, w=4),
+            )
             nc.vector.tensor_copy(gw[i][:], xw[:].bitcast(U32).indirect(lst[:]))
 
         g_ps = bank(7, "g_ps", [P, P])
@@ -153,8 +150,10 @@ def tile_picked_hkqmedsharepagex_none_po_kernel(
         for h in range(2):
             pair = slice(2 * h, 2 * h + 2)
             for t in (2 * h, 2 * h + 1):
-                gather(False, pa[:, t, :], a_win[t][:], n1_t[:])
-                gather(h == 0, pb[:, t, :], a_win[t][:], n2_t[:])
+                for c in range(CHUNKS):
+                    gather(False, pa[:, t, c * VC : (c + 1) * VC], a_win[t][:], n1_t[:, c * VC // 16 : (c + 1) * VC // 16])
+                for c in range(CHUNKS):
+                    gather(t == 0, pb[:, t, c * VC : (c + 1) * VC], a_win[t][:], n2_t[:, c * VC // 16 : (c + 1) * VC // 16])
                 nc.vector.tensor_copy(a_bf[:, t, :], a_win[t][:, :S])
             nc.vector.tensor_tensor(hi[:, pair, :], a_bf[:, pair, :], pa[:, pair, :], ALU.max)
             nc.vector.tensor_tensor(lo[:, pair, :], a_bf[:, pair, :], pa[:, pair, :], ALU.min)

@@ -54,7 +54,7 @@ def tile_picked_hkqmedsharepagex_none_po_kernel(
                 nc.vector.tensor_copy(out, window.indirect(offsets))
 
         xs = early.tile([P, T], U8, name="xs", align_bytes=64, offset=17408)
-        nc.vector.memset(xs[:].bitcast(I32), 0)
+        nc.gpsimd.memset(xs[:].bitcast(I32), 0)
         nc.sync.dma_start(xs[0:P:8, :].bitcast(I32), x_scales[0].bitcast(I32))
         offs_t = load_list("offs_t", offs)
         two_t = load_list("two_t", two)
@@ -86,7 +86,9 @@ def tile_picked_hkqmedsharepagex_none_po_kernel(
         nc.vector.memset(xsc[:].bitcast(I32), 0)
         ident = tile("ident", [P, P], F32)
         make_identity(nc, ident[:])
-        a_win = [tile("a_win%d" % t, [P, S], F32) for t in range(SLOTS)]
+        a_win = [tile("a_win%d" % t, [P, 2 * S], F32) for t in range(SLOTS)]
+        for t in range(SLOTS):
+            nc.vector.memset(a_win[t][:, S:], 0.0)
 
         nc.vector.tensor_copy(
             ws[0:16, :].bitcast(I32).rearrange("p (i t b w) -> p i t b w", i=2, t=SLOTS, w=2),
@@ -128,10 +130,9 @@ def tile_picked_hkqmedsharepagex_none_po_kernel(
             return acc
 
         ex = [tile("ex%d" % t, [P, V], F32) for t in range(SLOTS)]
-        a_bf = tile("a_bf", [P, SLOTS, S], BF16)
         for t in range(SLOTS):
             a_ps = first_product(0, t, "a_ps%d" % t)
-            nc.vector.tensor_scalar(a_win[t][:, :S], a_ps[:], ga_c[:, t : t + 1], None, ALU.mult)
+            nc.scalar.activation(a_win[t][:, :S], a_ps[:], ACT.Copy, scale=ga_c[:, t : t + 1])
             b_ps = first_product(1, t, "b_ps%d" % t)
             nc.scalar.activation(ex[t][:], b_ps[:], ACT.Exp, scale=0.5)
 
@@ -150,32 +151,35 @@ def tile_picked_hkqmedsharepagex_none_po_kernel(
         for h in range(2):
             pair = slice(2 * h, 2 * h + 2)
             for t in (2 * h, 2 * h + 1):
-                for c in range(CHUNKS):
-                    gather(False, pa[:, t, c * VC : (c + 1) * VC], a_win[t][:], n1_t[:, c * VC // 16 : (c + 1) * VC // 16])
-                for c in range(CHUNKS):
-                    gather(t == 0, pb[:, t, c * VC : (c + 1) * VC], a_win[t][:], n2_t[:, c * VC // 16 : (c + 1) * VC // 16])
-                nc.vector.tensor_copy(a_bf[:, t, :], a_win[t][:, :S])
-            nc.vector.tensor_tensor(hi[:, pair, :], a_bf[:, pair, :], pa[:, pair, :], ALU.max)
-            nc.vector.tensor_tensor(lo[:, pair, :], a_bf[:, pair, :], pa[:, pair, :], ALU.min)
-            nc.vector.tensor_tensor(mid[:, pair, :], hi[:, pair, :], pb[:, pair, :], ALU.min)
-            nc.vector.tensor_tensor(z_pl[:, pair, :], lo[:, pair, :], mid[:, pair, :], ALU.max)
+                gather(False, pa[:, t, :], a_win[t][:], n1_t[:])
+                gather(False, pb[:, t, :], a_win[t][:], n2_t[:])
+            nc.vector.tensor_tensor(hi[:, pair, :], pa[:, pair, :], pb[:, pair, :], ALU.max)
+            nc.vector.tensor_tensor(lo[:, pair, :], pa[:, pair, :], pb[:, pair, :], ALU.min)
+            for t in (2 * h, 2 * h + 1):
+                nc.vector.tensor_tensor(mid[:, t, :], a_win[t][:, :S], hi[:, t, :], ALU.min)
+            for t in (2 * h, 2 * h + 1):
+                nc.vector.tensor_tensor(z_pl[:, t, :], lo[:, t, :], mid[:, t, :], ALU.max)
         z_il = tile("z_il", [P, SLOTS * S], BF16)
-        nc.vector.tensor_copy(
-            z_il[:].rearrange("p (t a i s) -> p a t i s", t=SLOTS, i=2, s=SLOTS),
-            z_pl[:].rearrange("p s (a i t) -> p a t i s", t=SLOTS, i=2),
-        )
+        half = SLOTS * S // 2
+        for h in range(2):
+            nc.vector.tensor_copy(
+                z_il[:, h * half : (h + 1) * half].rearrange("p (t a i s) -> p a t i s", t=2, i=2, s=SLOTS),
+                z_pl[:].rearrange("p s (a i t) -> p a t i s", t=SLOTS, i=2)[:, :, 2 * h : 2 * h + 2, :, :],
+            )
         zq = tile("zq", [P, S], U32)
         zs = tile("zs", [P, S], U8)
-        nc.vector.quantize_mx(zq[:].bitcast(FP8X4), zs[:], z_il[:])
+        for h in range(2):
+            cols = slice(h * S // 2, (h + 1) * S // 2)
+            nc.vector.quantize_mx(zq[:, cols].bitcast(FP8X4), zs[:, cols], z_il[:, h * half : (h + 1) * half])
 
-        def denominators(c):
+        def root_of_denominators(c):
             cols = slice(c * VC // 16, (c + 1) * VC // 16)
             g3 = tile("g3_%d" % c, [P, SLOTS, VC], F32)
             g4 = tile("g4_%d" % c, [P, SLOTS, VC], F32)
             for t in range(SLOTS):
                 gather(True, g3[:, t, :], ex[t][:], n3_t[:, cols])
                 gather(True, g4[:, t, :], ex[t][:], n4_t[:, cols])
-            r_t = []
+            roots = []
             for vb in range(2):
                 den = bank(4 * c + vb, "den%d_%d" % (c, vb), [P, SLOTS, P])
                 for t in range(SLOTS):
@@ -185,41 +189,50 @@ def tile_picked_hkqmedsharepagex_none_po_kernel(
                         nc.tensor.matmul(den[:, t, :], term, ident[:], start=(n == 0), stop=(n == 2), is_transpose=True)
                 rt = tile("rt%d_%d" % (c, vb), [P, SLOTS, P], F32)
                 nc.scalar.activation(rt[:], den[:], ACT.Abs_reciprocal_sqrt)
-                rt2 = tile("rt2_%d_%d" % (c, vb), [P, SLOTS, P], F32)
-                nc.scalar.activation(rt2[:], rt[:], ACT.Square)
-                r_t.append(rt2)
-            r_ps = []
-            for h in range(2):
-                r = bank(4 + 2 * c + h, "r%d_%d" % (c, h), [P, 2, VC])
-                for tt in range(2):
-                    for vb in range(2):
-                        nc.tensor.transpose(r[:, tt, vb * P : (vb + 1) * P], r_t[vb][:, 2 * h + tt, :], ident[:])
-                r_ps.append(r)
-            return r_ps
+                roots.append(rt)
+            return roots
 
-        def second_factor(c, r_ps):
-            z2_pl = sb.tile([P, SLOTS, VC], BF16, name="z2_pl%d" % c, tag="z2_pl%d" % c, align_bytes=64)
+        def turn_back(c, vb, src):
+            r = bank(4 + 2 * c + vb, "r%d_%d" % (c, vb), [P, SLOTS, P])
             for t in range(SLOTS):
-                nc.vector.scalar_tensor_tensor(
-                    z2_pl[:, t, :], ex[t][:, c * VC : (c + 1) * VC], gb2_c[:, t : t + 1], r_ps[t // 2][:, t % 2, :], ALU.mult, ALU.mult
-                )
+                nc.tensor.transpose(r[:, t, :], src[:, t, :], ident[:])
+            return r
+
+        def quantise_second_factor(c, u, r_ps):
             z2_il = sb.tile([P, VC, SLOTS], BF16, name="z2_il%d" % c, tag="z2_il%d" % c, align_bytes=64)
-            dst = z2_il[:].rearrange("p (a i) s -> p a s i", i=4)
-            src = z2_pl[:].rearrange("p s (a i) -> p a s i", i=4)
-            if c == 0:
-                nc.vector.tensor_copy(dst, src)
-            else:
-                nc.scalar.copy(dst, src)
+            for vb in range(2):
+                nc.vector.tensor_tensor(
+                    z2_il[:, vb * P : (vb + 1) * P, :].rearrange("p (a i) s -> p a s i", i=4),
+                    r_ps[vb][:].rearrange("p s (a i) -> p a s i", i=4),
+                    u[:, vb, :, :].rearrange("p s (a i) -> p a s i", i=4),
+                    ALU.mult,
+                )
             z2q = tile("z2q%d" % c, [P, VC], U32)
             z2s = tile("z2s%d" % c, [P, VC], U8)
-            nc.vector.quantize_mx(z2q[:].bitcast(FP8X4), z2s[:], z2_il[:].rearrange("p v s -> p (v s)"))
+            for vb in range(2):
+                cols = slice(vb * P, (vb + 1) * P)
+                nc.vector.quantize_mx(z2q[:, cols].bitcast(FP8X4), z2s[:, cols], z2_il[:, cols, :].rearrange("p v s -> p (v s)"))
             return z2q, z2s
+
+        def second_factor(c):
+            roots = root_of_denominators(c)
+            r_ps = []
+            for vb in range(2):
+                sq = tile("sq%d_%d" % (c, vb), [P, SLOTS, P], F32)
+                nc.scalar.activation(sq[:], roots[vb][:], ACT.Square)
+                r_ps.append(turn_back(c, vb, sq))
+            u = tile("u%d" % c, [P, 2, SLOTS, P], F32)
+            for t in range(SLOTS):
+                nc.scalar.activation(
+                    u[:, :, t, :], ex[t][:, c * VC : (c + 1) * VC].rearrange("p (b v) -> p b v", b=2), ACT.Copy, scale=gb2_c[:, t : t + 1]
+                )
+            return quantise_second_factor(c, u, r_ps)
 
         y_pl = tile("y_pl", [P, SLOTS, U], BF16)
 
-        def write_page(c, halves, z2q, z2s):
-            cols = slice(c * VC // 16, (c + 1) * VC // 16)
-            for h in halves:
+        def scores(c, z2q, z2s):
+            banks = []
+            for h in range(2):
                 s_ps = bank(2 * c + h, "s%d_%d" % (c, h), [P, 2, VC])
                 for tt in range(2):
                     t = 2 * h + tt
@@ -231,54 +244,57 @@ def tile_picked_hkqmedsharepagex_none_po_kernel(
                         rhs_scale=z2s[:],
                         start=True, stop=True,
                     )
-                for tt in range(2):
-                    t = 2 * h + tt
-                    tag = {(0, 2): "ex3", (0, 3): "z2_il1"}.get((c, t), "nw%d_%d" % (c, t))
-                    nw = sb.tile([P, VC], F32, name="nw%d_%d" % (c, t), tag=tag, align_bytes=64)
-                    nc.vector.scalar_tensor_tensor(
-                        nw[:], s_ps[:, tt, :], 0.0625, held[:, t, c * VC : (c + 1) * VC], ALU.mult, ALU.max
-                    )
-                    nc.vector.tensor_copy(page[t][:].indirect(n5_t[:, cols]), nw[:])
-                    if c == CHUNKS - 1:
-                        nc.sync.dma_start(out_v[:, t, :], page[t][:])
-                        if t < SLOTS - 1:
-                            nc.scalar.copy(y_pl[:, t, :], page[t][:])
-                        else:
-                            nc.vector.tensor_copy(y_pl[:, t, : U // 2], page[t][:, : U // 2])
-                            nc.scalar.copy(y_pl[:, t, U // 2 :], page[t][:, U // 2 :])
+                banks.append(s_ps)
+            return banks
+
+        def write_page(c, t0, t1, s_banks, tag):
+            cols = slice(c * VC // 16, (c + 1) * VC // 16)
+            nw = sb.tile([P, t1 - t0, VC], F32, name="nw%d_%d" % (c, t0), tag=tag, align_bytes=64)
+            nc.vector.scalar_tensor_tensor(
+                nw[:], s_banks[t0 // 2][:, t0 % 2 : t0 % 2 + t1 - t0, :], 0.0625, held[:, t0:t1, c * VC : (c + 1) * VC], ALU.mult, ALU.max
+            )
+            for t in range(t0, t1):
+                nc.vector.tensor_copy(page[t][:].indirect(n5_t[:, cols]), nw[:, t - t0, :])
+                if c == CHUNKS - 1:
+                    nc.sync.dma_start(out_v[:, t, :], page[t][:])
+                    if t < SLOTS - 1:
+                        nc.scalar.copy(y_pl[:, t, :], page[t][:])
+                    else:
+                        nc.vector.tensor_copy(y_pl[:, t, : U // 2], page[t][:, : U // 2])
+                        nc.scalar.copy(y_pl[:, t, U // 2 :], page[t][:, U // 2 :])
 
         held = tile("held", [P, SLOTS, V], F32)
 
         def hold(t):
             nc.scalar.activation(held[:, t, :], page[t][:].indirect(n5_t[:]), ACT.Copy, scale=0.5)
 
-        z2_0 = second_factor(0, denominators(0))
-        hold(0)
-        hold(1)
-        write_page(0, (0,), *z2_0)
-        hold(2)
-        hold(3)
-        z2_1 = second_factor(1, denominators(1))
-        write_page(0, (1,), *z2_0)
-        write_page(1, (0, 1), *z2_1)
+        s_0 = scores(0, *second_factor(0))
+        for t in range(SLOTS):
+            hold(t)
+        write_page(0, 0, 2, s_0, "nw0_0")
+        write_page(0, 2, 3, s_0, "nw0_2")
+        s_1 = scores(1, *second_factor(1))
+        write_page(0, 3, 4, s_0, "z2_il1")
+        write_page(1, 0, 2, s_1, "nw1_0")
+        write_page(1, 2, 4, s_1, "nw1_2")
 
         ys = tile("ys", [P, U], U8)
         words_v = out_1[0].rearrange("p n t -> p (n t)").bitcast(I32)
-        yq = [tile("yq%d" % h, [P, U // 2], U32) for h in range(2)]
+        y_il = [tile("y_il%d" % n, [P, UQ, SLOTS], BF16) for n in range(QUARTERS)]
         for n in range(QUARTERS):
-            cols = slice(n * UQ, (n + 1) * UQ)
-            y_il = tile("y_il%d" % n, [P, UQ, SLOTS], BF16)
-            dst = y_il[:].rearrange("p (a i) s -> p a s i", i=4)
-            src = y_pl[:, :, cols].rearrange("p s (a i) -> p a s i", i=4)
+            dst = y_il[n][:].rearrange("p (a i) s -> p a s i", i=4)
+            src = y_pl[:, :, n * UQ : (n + 1) * UQ].rearrange("p s (a i) -> p a s i", i=4)
             if n < 2:
                 nc.vector.tensor_copy(dst, src)
             else:
                 nc.scalar.copy(dst, src)
-            nc.vector.quantize_mx(
-                yq[n // 2][:, (n % 2) * UQ : (n % 2 + 1) * UQ].bitcast(FP8X4), ys[:, cols], y_il[:].rearrange("p v s -> p (v s)")
-            )
-            if n % 2 == 1:
-                h = n // 2
-                nc.sync.dma_start(words_v[:, h * U // 2 : (h + 1) * U // 2], yq[h][:].bitcast(I32))
+        for n0, n1q in ((0, 2), (2, 3), (3, 4)):
+            yq = tile("yq%d" % n0, [P, (n1q - n0) * UQ], U32)
+            for n in range(n0, n1q):
+                nc.vector.quantize_mx(
+                    yq[:, (n - n0) * UQ : (n - n0 + 1) * UQ].bitcast(FP8X4), ys[:, n * UQ : (n + 1) * UQ], y_il[n][:].rearrange("p v s -> p (v s)")
+                )
+            nc.sync.dma_start(words_v[:, n0 * UQ : n1q * UQ], yq[:].bitcast(I32))
         for q in range(4):
-            nc.sync.dma_start(out_2[0, 4 * q : 4 * q + 4, :].bitcast(I32), ys[32 * q : 32 * q + 4, :].bitcast(I32))
+            queue = nc.sync if q < 2 else nc.scalar
+            queue.dma_start(out_2[0, 4 * q : 4 * q + 4, :].bitcast(I32), ys[32 * q : 32 * q + 4, :].bitcast(I32))

@@ -53,17 +53,18 @@ def tile_picked_hkqmedsharepagex_none_po_kernel(
             else:
                 nc.vector.tensor_copy(out, window.indirect(offsets))
 
-        xs = early.tile([P, T], U8, name="xs", align_bytes=64, offset=17408)
+        xs = early.tile([P, T], U8, name="xs", align_bytes=64, offset=5 * 4096)
         nc.gpsimd.memset(xs[:].bitcast(I32), 0)
-        nc.sync.dma_start(xs[0:P:8, :].bitcast(I32), x_scales[0].bitcast(I32))
+        for e in range(2):
+            nc.sync.dma_start(xs[e:P:16, :].bitcast(I32), x_scales[0, e:16:2, :].bitcast(I32))
         offs_t = load_list("offs_t", offs)
         two_t = load_list("two_t", two)
         ws_raw = tile("ws_raw", [16, 2 * H], U8)
         for i, src in enumerate((w1_scales, w2_scales)):
             nc.sync.dma_start(ws_raw[:, i * H : (i + 1) * H].bitcast(I32), src[0].bitcast(I32))
-        w_raw = [early.tile([P, 2 * H], U8, name="w_raw%d" % i, align_bytes=64, offset=1024 * i) for i in range(2)]
+        w_raw = [tile("w_raw%d" % i, [P, 2 * H], U8) for i in range(2)]
         nc.sync.dma_start(w_raw[0][:].bitcast(I32), w1_words[0].bitcast(I32))
-        xw = early.tile([P, T], I32, name="xw", align_bytes=64, offset=8192)
+        xw = tile("xw", [P, T], I32)
         nc.sync.dma_start(xw[:], x_words[0].rearrange("p n t -> p (n t)").bitcast(I32))
         nc.sync.dma_start(w_raw[1][:].bitcast(I32), w2_words[0].bitcast(I32))
         n1_t = load_list("n1_t", n1)
@@ -72,7 +73,7 @@ def tile_picked_hkqmedsharepagex_none_po_kernel(
         n4_t = load_list("n4_t", n4)
         n5_t = load_list("n5_t", n5)
 
-        w_dealt = [tile("w_dealt%d" % i, [P, 2 * H], U8) for i in range(2)]
+        w_dealt = [early.tile([P, 2 * H], U8, name="w_dealt%d" % i, align_bytes=64, offset=(7 - 4 * i) * 4096 - 512) for i in range(2)]
         g_rows = tile("g_rows", [P, P], F32)
         nc.vector.memset(g_rows[:], 0.0)
         for i, factor in enumerate((ga, gb)):
@@ -82,8 +83,6 @@ def tile_picked_hkqmedsharepagex_none_po_kernel(
             )
         ws = tile("ws", [P, 2 * H], U8)
         nc.vector.memset(ws[:].bitcast(I32), 0)
-        xsc = tile("xsc", [P, 2 * S], U8)
-        nc.vector.memset(xsc[:].bitcast(I32), 0)
         ident = tile("ident", [P, P], F32)
         make_identity(nc, ident[:])
         a_win = [tile("a_win%d" % t, [P, 2 * S], F32) for t in range(SLOTS)]
@@ -97,12 +96,14 @@ def tile_picked_hkqmedsharepagex_none_po_kernel(
         for q in range(1, 4):
             nc.scalar.dma_start(ws[32 * q : 32 * q + 4, :].bitcast(I32), ws[4 * q : 4 * q + 4, :].bitcast(I32))
 
-        gs = early.tile([P, 2 * S], U8, name="gs", align_bytes=64, offset=4096)
+        gs = [tile("gs0", [P, S], U8), early.tile([P, S], U8, name="gs1", align_bytes=64, offset=4096 - 256)]
+        xsc = [tile("xsc%d" % i, [P, S], U8) for i in range(2)]
         for i, lst in enumerate((offs_t, two_t)):
-            nc.vector.tensor_copy(gs[:, i * S : (i + 1) * S], xs[:].indirect(lst[:]))
-        for r in range(4):
-            nc.scalar.dma_start(xsc[r:P:32, :].bitcast(I32), gs[8 * r : P : 32, :].bitcast(I32))
-        gw = [early.tile([P, S], U32, name="gw%d" % i, align_bytes=64, offset=16384 + 2048 * i) for i in range(2)]
+            nc.vector.tensor_copy(gs[i][:], xs[:].indirect(lst[:]))
+            nc.vector.tensor_copy(xsc[i][:].bitcast(I32), gs[i][:].bitcast(I32))
+            for e in range(2):
+                nc.scalar.dma_start(xsc[i][2 + e : P : 32, :].bitcast(I32), gs[i][16 + e : P : 32, :].bitcast(I32))
+        gw = [early.tile([P, S], U32, name="gw%d" % i, align_bytes=64, offset=5 * 4096 - 1024 + 2048 * i) for i in range(2)]
         for i, lst in enumerate((offs_t, two_t)):
             nc.vector.tensor_copy(
                 w_dealt[i][:].bitcast(I32).rearrange("p (t b w) -> p t b w", t=SLOTS, w=4),
@@ -124,7 +125,7 @@ def tile_picked_hkqmedsharepagex_none_po_kernel(
                 lhsT=w_dealt[i][:, 2 * P * t : 2 * P * (t + 1)].bitcast(FP4X4),
                 lhsT_scale=ws[:, i * H + P * t : i * H + P * (t + 1)],
                 rhs=gw[i][:].bitcast(FP8X4),
-                rhs_scale=xsc[:, i * S : (i + 1) * S],
+                rhs_scale=xsc[i][:],
                 start=True, stop=True,
             )
             return acc
@@ -136,11 +137,13 @@ def tile_picked_hkqmedsharepagex_none_po_kernel(
             b_ps = first_product(1, t, "b_ps%d" % t)
             nc.scalar.activation(ex[t][:], b_ps[:], ACT.Exp, scale=0.5)
 
-        page = [early.tile([P, U], F32, name="page%d" % t, align_bytes=64, offset=4096 * t) for t in range(SLOTS)]
+        old = [early.tile([P, U], F32, name="old%d" % t, align_bytes=64, offset=4096 * t) for t in range(SLOTS)]
+        page = [early.tile([P, U], F32, name="page%d" % t, align_bytes=64, offset=4096 * (SLOTS + t)) for t in range(SLOTS)]
         mem_v = mem.rearrange("(p t) u -> p t u", t=SLOTS)
         out_v = out_0.rearrange("(p t) u -> p t u", t=SLOTS)
-        for t in range(SLOTS):
-            nc.sync.dma_start(page[t][:], mem_v[:, t, :])
+        for dst in (old, page):
+            for t in range(SLOTS):
+                nc.sync.dma_start(dst[t][:], mem_v[:, t, :])
 
         pa = tile("pa", [P, SLOTS, S], BF16)
         pb = tile("pb", [P, SLOTS, S], BF16)
@@ -247,11 +250,18 @@ def tile_picked_hkqmedsharepagex_none_po_kernel(
                 banks.append(s_ps)
             return banks
 
-        def write_page(c, t0, t1, s_banks, tag):
+        def halved_old(c, t0, t1, tag):
+            cols = slice(c * VC // 16, (c + 1) * VC // 16)
+            held = sb.tile([P, t1 - t0, VC], F32, name="held%d_%d" % (c, t0), tag=tag, align_bytes=64)
+            for t in range(t0, t1):
+                nc.scalar.activation(held[:, t - t0, :], old[t][:].indirect(n5_t[:, cols]), ACT.Copy, scale=0.5)
+            return held
+
+        def write_page(c, t0, t1, s_banks, held, tag):
             cols = slice(c * VC // 16, (c + 1) * VC // 16)
             nw = sb.tile([P, t1 - t0, VC], F32, name="nw%d_%d" % (c, t0), tag=tag, align_bytes=64)
             nc.vector.scalar_tensor_tensor(
-                nw[:], s_banks[t0 // 2][:, t0 % 2 : t0 % 2 + t1 - t0, :], 0.0625, held[:, t0:t1, c * VC : (c + 1) * VC], ALU.mult, ALU.max
+                nw[:], s_banks[t0 // 2][:, t0 % 2 : t0 % 2 + t1 - t0, :], 0.0625, held[:], ALU.mult, ALU.max
             )
             for t in range(t0, t1):
                 nc.vector.tensor_copy(page[t][:].indirect(n5_t[:, cols]), nw[:, t - t0, :])
@@ -263,20 +273,13 @@ def tile_picked_hkqmedsharepagex_none_po_kernel(
                         nc.vector.tensor_copy(y_pl[:, t, : U // 2], page[t][:, : U // 2])
                         nc.scalar.copy(y_pl[:, t, U // 2 :], page[t][:, U // 2 :])
 
-        held = tile("held", [P, SLOTS, V], F32)
-
-        def hold(t):
-            nc.scalar.activation(held[:, t, :], page[t][:].indirect(n5_t[:]), ACT.Copy, scale=0.5)
-
         s_0 = scores(0, *second_factor(0))
-        for t in range(SLOTS):
-            hold(t)
-        write_page(0, 0, 2, s_0, "nw0_0")
-        write_page(0, 2, 3, s_0, "nw0_2")
+        write_page(0, 0, 2, s_0, halved_old(0, 0, 2, "held0_0"), "nw0_0")
+        write_page(0, 2, 3, s_0, halved_old(0, 2, 3, "held0_2"), "nw0_2")
         s_1 = scores(1, *second_factor(1))
-        write_page(0, 3, 4, s_0, "z2_il1")
-        write_page(1, 0, 2, s_1, "nw1_0")
-        write_page(1, 2, 4, s_1, "nw1_2")
+        write_page(0, 3, 4, s_0, halved_old(0, 3, 4, "rt1_1"), "z2_il1")
+        write_page(1, 0, 2, s_1, halved_old(1, 0, 2, "sq1_0"), "nw1_0")
+        write_page(1, 2, 4, s_1, halved_old(1, 2, 4, "sq1_1"), "nw1_2")
 
         ys = tile("ys", [P, U], U8)
         words_v = out_1[0].rearrange("p n t -> p (n t)").bitcast(I32)

@@ -73,22 +73,31 @@ def tile_picked_hkqmedsharepagex_none_po_kernel(
         n4_t = load_list("n4_t", n4)
         n5_t = load_list("n5_t", n5)
 
-        w_dealt = [early.tile([P, 2 * H], U8, name="w_dealt%d" % i, align_bytes=64, offset=(7 - 4 * i) * 4096 - 512) for i in range(2)]
-        g_rows = tile("g_rows", [P, P], F32)
-        nc.vector.memset(g_rows[:], 0.0)
+        g_rows = early.tile([P, P], F32, name="g_rows", align_bytes=64, offset=7 * 4096 - 256)
+        nc.gpsimd.memset(g_rows[:], 0.0)
         for i, factor in enumerate((ga, gb)):
             nc.gpsimd.dma_start(
                 g_rows[SLOTS * i : SLOTS * (i + 1), :].rearrange("t (b q) -> t b q", q=8),
                 factor.rearrange("(b t q) o -> t b (q o)", t=SLOTS, q=8),
             )
-        ws = tile("ws", [P, 2 * H], U8)
+        ws = early.tile([P, 2 * H], U8, name="ws", align_bytes=64, offset=3 * 4096 - 512)
         nc.vector.memset(ws[:].bitcast(I32), 0)
         ident = tile("ident", [P, P], F32)
         make_identity(nc, ident[:])
         a_win = [tile("a_win%d" % t, [P, 2 * S], F32) for t in range(SLOTS)]
         for t in range(SLOTS):
             nc.vector.memset(a_win[t][:, S:], 0.0)
+        warm = tile("warm", [P, 1], F32)
+        nc.scalar.activation(warm[:], a_win[0][:, S : S + 1], ACT.Exp)
 
+        g_ps = bank(7, "g_ps", [P, P])
+        nc.tensor.transpose(g_ps[:], g_rows[:], ident[:])
+        ga_c = tile("ga_c", [P, SLOTS], F32)
+        gb2_c = tile("gb2_c", [P, SLOTS], F32)
+        nc.scalar.copy(ga_c[:], g_ps[:, 0:SLOTS])
+        nc.scalar.activation(gb2_c[:], g_ps[:, SLOTS : 2 * SLOTS], ACT.Copy, scale=2.0)
+
+        w_dealt = [early.tile([P, 2 * H], U8, name="w_dealt%d" % i, align_bytes=64, offset=7 * 4096 - 1024 * (1 - i)) for i in range(2)]
         nc.vector.tensor_copy(
             ws[0:16, :].bitcast(I32).rearrange("p (i t b w) -> p i t b w", i=2, t=SLOTS, w=2),
             ws_raw[:].bitcast(I32).rearrange("p (i b t w) -> p i t b w", i=2, t=SLOTS, w=2),
@@ -111,13 +120,6 @@ def tile_picked_hkqmedsharepagex_none_po_kernel(
             )
             nc.vector.tensor_copy(gw[i][:], xw[:].bitcast(U32).indirect(lst[:]))
 
-        g_ps = bank(7, "g_ps", [P, P])
-        nc.tensor.transpose(g_ps[:], g_rows[:], ident[:])
-        ga_c = tile("ga_c", [P, SLOTS], F32)
-        gb2_c = tile("gb2_c", [P, SLOTS], F32)
-        nc.vector.tensor_copy(ga_c[:], g_ps[:, 0:SLOTS])
-        nc.vector.tensor_scalar(gb2_c[:], g_ps[:, SLOTS : 2 * SLOTS], 2.0, None, ALU.mult)
-
         def first_product(i, t, name):
             acc = bank(SLOTS * i + t, name, [P, S])
             nc.tensor.matmul_mx(
@@ -133,7 +135,10 @@ def tile_picked_hkqmedsharepagex_none_po_kernel(
         ex = [tile("ex%d" % t, [P, V], F32) for t in range(SLOTS)]
         for t in range(SLOTS):
             a_ps = first_product(0, t, "a_ps%d" % t)
-            nc.scalar.activation(a_win[t][:, :S], a_ps[:], ACT.Copy, scale=ga_c[:, t : t + 1])
+            if t == 0:
+                nc.vector.tensor_scalar(a_win[t][:, :S], a_ps[:], ga_c[:, t : t + 1], None, ALU.mult)
+            else:
+                nc.scalar.activation(a_win[t][:, :S], a_ps[:], ACT.Copy, scale=ga_c[:, t : t + 1])
             b_ps = first_product(1, t, "b_ps%d" % t)
             nc.scalar.activation(ex[t][:], b_ps[:], ACT.Exp, scale=0.5)
 
@@ -162,18 +167,17 @@ def tile_picked_hkqmedsharepagex_none_po_kernel(
                 nc.vector.tensor_tensor(mid[:, t, :], a_win[t][:, :S], hi[:, t, :], ALU.min)
             for t in (2 * h, 2 * h + 1):
                 nc.vector.tensor_tensor(z_pl[:, t, :], lo[:, t, :], mid[:, t, :], ALU.max)
-        z_il = tile("z_il", [P, SLOTS * S], BF16)
-        half = SLOTS * S // 2
+        z_il = [tile("z_il%d" % h, [P, SLOTS * S // 2], BF16) for h in range(2)]
         for h in range(2):
             nc.vector.tensor_copy(
-                z_il[:, h * half : (h + 1) * half].rearrange("p (t a i s) -> p a t i s", t=2, i=2, s=SLOTS),
+                z_il[h][:].rearrange("p (t a i s) -> p a t i s", t=2, i=2, s=SLOTS),
                 z_pl[:].rearrange("p s (a i t) -> p a t i s", t=SLOTS, i=2)[:, :, 2 * h : 2 * h + 2, :, :],
             )
         zq = tile("zq", [P, S], U32)
         zs = tile("zs", [P, S], U8)
         for h in range(2):
             cols = slice(h * S // 2, (h + 1) * S // 2)
-            nc.vector.quantize_mx(zq[:, cols].bitcast(FP8X4), zs[:, cols], z_il[:, h * half : (h + 1) * half])
+            nc.vector.quantize_mx(zq[:, cols].bitcast(FP8X4), zs[:, cols], z_il[h][:])
 
         def root_of_denominators(c):
             cols = slice(c * VC // 16, (c + 1) * VC // 16)
@@ -201,22 +205,6 @@ def tile_picked_hkqmedsharepagex_none_po_kernel(
                 nc.tensor.transpose(r[:, t, :], src[:, t, :], ident[:])
             return r
 
-        def quantise_second_factor(c, u, r_ps):
-            z2_il = sb.tile([P, VC, SLOTS], BF16, name="z2_il%d" % c, tag="z2_il%d" % c, align_bytes=64)
-            for vb in range(2):
-                nc.vector.tensor_tensor(
-                    z2_il[:, vb * P : (vb + 1) * P, :].rearrange("p (a i) s -> p a s i", i=4),
-                    r_ps[vb][:].rearrange("p s (a i) -> p a s i", i=4),
-                    u[:, vb, :, :].rearrange("p s (a i) -> p a s i", i=4),
-                    ALU.mult,
-                )
-            z2q = tile("z2q%d" % c, [P, VC], U32)
-            z2s = tile("z2s%d" % c, [P, VC], U8)
-            for vb in range(2):
-                cols = slice(vb * P, (vb + 1) * P)
-                nc.vector.quantize_mx(z2q[:, cols].bitcast(FP8X4), z2s[:, cols], z2_il[:, cols, :].rearrange("p v s -> p (v s)"))
-            return z2q, z2s
-
         def second_factor(c):
             roots = root_of_denominators(c)
             r_ps = []
@@ -229,11 +217,26 @@ def tile_picked_hkqmedsharepagex_none_po_kernel(
                 nc.scalar.activation(
                     u[:, :, t, :], ex[t][:, c * VC : (c + 1) * VC].rearrange("p (b v) -> p b v", b=2), ACT.Copy, scale=gb2_c[:, t : t + 1]
                 )
-            return quantise_second_factor(c, u, r_ps)
+            z2_il = [tile("z2_il%d_%d" % (c, vb), [P, SLOTS * P], BF16) for vb in range(2)]
+            for vb in range(2):
+                nc.vector.tensor_tensor(
+                    z2_il[vb][:].rearrange("p (a i s) -> p a s i", i=4, s=SLOTS),
+                    r_ps[vb][:].rearrange("p s (a i) -> p a s i", i=4),
+                    u[:, vb, :, :].rearrange("p s (a i) -> p a s i", i=4),
+                    ALU.mult,
+                )
+            return z2_il
+
+        z2q = [tile("z2q%d" % c, [P, VC], U32) for c in range(CHUNKS)]
+        z2s = [tile("z2s%d" % c, [P, VC], U8) for c in range(CHUNKS)]
+
+        def quantise_block(c, vb, z2_il):
+            cols = slice(vb * P, (vb + 1) * P)
+            nc.vector.quantize_mx(z2q[c][:, cols].bitcast(FP8X4), z2s[c][:, cols], z2_il[vb][:])
 
         y_pl = tile("y_pl", [P, SLOTS, U], BF16)
 
-        def scores(c, z2q, z2s):
+        def scores(c):
             banks = []
             for h in range(2):
                 s_ps = bank(2 * c + h, "s%d_%d" % (c, h), [P, 2, VC])
@@ -243,8 +246,8 @@ def tile_picked_hkqmedsharepagex_none_po_kernel(
                         s_ps[:, tt, :],
                         lhsT=zq[:, P * t : P * (t + 1)].bitcast(FP8X4),
                         lhsT_scale=zs[:, P * t : P * (t + 1)],
-                        rhs=z2q[:].bitcast(FP8X4),
-                        rhs_scale=z2s[:],
+                        rhs=z2q[c][:].bitcast(FP8X4),
+                        rhs_scale=z2s[c][:],
                         start=True, stop=True,
                     )
                 banks.append(s_ps)
@@ -257,12 +260,15 @@ def tile_picked_hkqmedsharepagex_none_po_kernel(
                 nc.scalar.activation(held[:, t - t0, :], old[t][:].indirect(n5_t[:, cols]), ACT.Copy, scale=0.5)
             return held
 
-        def write_page(c, t0, t1, s_banks, held, tag):
-            cols = slice(c * VC // 16, (c + 1) * VC // 16)
+        def new_values(c, t0, t1, s_banks, held, tag):
             nw = sb.tile([P, t1 - t0, VC], F32, name="nw%d_%d" % (c, t0), tag=tag, align_bytes=64)
             nc.vector.scalar_tensor_tensor(
                 nw[:], s_banks[t0 // 2][:, t0 % 2 : t0 % 2 + t1 - t0, :], 0.0625, held[:], ALU.mult, ALU.max
             )
+            return nw
+
+        def write_page(c, t0, t1, nw):
+            cols = slice(c * VC // 16, (c + 1) * VC // 16)
             for t in range(t0, t1):
                 nc.vector.tensor_copy(page[t][:].indirect(n5_t[:, cols]), nw[:, t - t0, :])
                 if c == CHUNKS - 1:
@@ -270,16 +276,28 @@ def tile_picked_hkqmedsharepagex_none_po_kernel(
                     if t < SLOTS - 1:
                         nc.scalar.copy(y_pl[:, t, :], page[t][:])
                     else:
-                        nc.vector.tensor_copy(y_pl[:, t, : U // 2], page[t][:, : U // 2])
+                        for n in range(2):
+                            nc.vector.tensor_copy(y_pl[:, t, n * UQ : (n + 1) * UQ], page[t][:, n * UQ : (n + 1) * UQ])
                         nc.scalar.copy(y_pl[:, t, U // 2 :], page[t][:, U // 2 :])
 
-        s_0 = scores(0, *second_factor(0))
-        write_page(0, 0, 2, s_0, halved_old(0, 0, 2, "held0_0"), "nw0_0")
-        write_page(0, 2, 3, s_0, halved_old(0, 2, 3, "held0_2"), "nw0_2")
-        s_1 = scores(1, *second_factor(1))
-        write_page(0, 3, 4, s_0, halved_old(0, 3, 4, "rt1_1"), "z2_il1")
-        write_page(1, 0, 2, s_1, halved_old(1, 0, 2, "sq1_0"), "nw1_0")
-        write_page(1, 2, 4, s_1, halved_old(1, 2, 4, "sq1_1"), "nw1_2")
+        z2_il = second_factor(0)
+        for vb in range(2):
+            quantise_block(0, vb, z2_il)
+        s_0 = scores(0)
+        nw_a = new_values(0, 0, 2, s_0, halved_old(0, 0, 2, "held0_0"), "nw0_0")
+        nw_b = new_values(0, 2, 3, s_0, halved_old(0, 2, 3, "held0_2"), "nw0_2")
+        write_page(0, 0, 2, nw_a)
+        write_page(0, 2, 3, nw_b)
+        z2_il = second_factor(1)
+        quantise_block(1, 0, z2_il)
+        nw_c = new_values(0, 3, 4, s_0, halved_old(0, 3, 4, "rt1_1"), "u1")
+        quantise_block(1, 1, z2_il)
+        s_1 = scores(1)
+        write_page(0, 3, 4, nw_c)
+        nw_a = new_values(1, 0, 2, s_1, halved_old(1, 0, 2, "sq1_0"), "nw1_0")
+        nw_b = new_values(1, 2, 4, s_1, halved_old(1, 2, 4, "sq1_1"), "nw1_2")
+        write_page(1, 0, 2, nw_a)
+        write_page(1, 2, 4, nw_b)
 
         ys = tile("ys", [P, U], U8)
         words_v = out_1[0].rearrange("p n t -> p (n t)").bitcast(I32)

from contextlib import ExitStack

import concourse.mybir as mybir
from concourse.masks import make_identity

K, T, S, V, H, U = 512, 2048, 512, 512, 512, 1024
P = 128
SLOTS = 4
FLOPS = 3 * 2 * 512 * 512 * 512

F32 = mybir.dt.float32
BF16 = mybir.dt.bfloat16
I32 = mybir.dt.int32
U32 = mybir.dt.uint32
U16 = mybir.dt.uint16
U8 = mybir.dt.uint8
FP8X4 = mybir.dt.float8_e4m3fn_x4
FP4X4 = mybir.dt.float4_e2m1fn_x4
ALU = mybir.AluOpType
ACT = mybir.ActivationFunctionType

CHUNKS = 2
VC = V // CHUNKS
QUARTERS = 4
UQ = U // QUARTERS


def tile_picked_hkqmedsharepagex_none_po_kernel(
    tc, x_words, x_scales, w1_words, w1_scales, w2_words, w2_scales, ga, gb, mem,
    offs, two, n1, n2, n3, n4, n5, out_0, out_1, out_2,
):
    nc = tc.nc
    with ExitStack() as ctx:
        lists = ctx.enter_context(tc.tile_pool(name="lists", bufs=1))
        sb = ctx.enter_context(tc.tile_pool(name="sb", bufs=1))
        early = ctx.enter_context(tc.tile_pool(name="early", bufs=1))
        psum = ctx.enter_context(tc.psum_pool(name="psum", bufs=1))

        def tile(name, shape, dtype):
            return sb.tile(shape, dtype, name=name, align_bytes=64)

        def bank(i, name, shape):
            return psum.tile(shape, F32, name=name, tag="bank%d" % i)

        def load_list(name, src):
            t = lists.tile([P, 32], U16, name=name)
            nc.sync.dma_start(t[:], src)
            return t

        def gather(on_scalar, out, window, offsets):
            if on_scalar:
                nc.scalar.activation(out, window.indirect(offsets), ACT.Copy)
            else:
                nc.vector.tensor_copy(out, window.indirect(offsets))

        xs = early.tile([P, T], U8, name="xs", align_bytes=64, offset=5 * 4096)
        nc.gpsimd.memset(xs[:].bitcast(I32), 0)
        for e in range(2):
            nc.sync.dma_start(xs[e:P:16, :].bitcast(I32), x_scales[0, e:16:2, :].bitcast(I32))
        offs_t = load_list("offs_t", offs)
        two_t = load_list("two_t", two)
        ws_raw = tile("ws_raw", [16, 2 * H], U8)
        for i, src in enumerate((w1_scales, w2_scales)):
            nc.sync.dma_start(ws_raw[:, i * H : (i + 1) * H].bitcast(I32), src[0].bitcast(I32))
        w_raw = [tile("w_raw%d" % i, [P, 2 * H], U8) for i in range(2)]
        nc.sync.dma_start(w_raw[0][:].bitcast(I32), w1_words[0].bitcast(I32))
        xw = tile("xw", [P, T], I32)
        nc.sync.dma_start(xw[:], x_words[0].rearrange("p n t -> p (n t)").bitcast(I32))
        nc.sync.dma_start(w_raw[1][:].bitcast(I32), w2_words[0].bitcast(I32))
        n1_t = load_list("n1_t", n1)
        n2_t = load_list("n2_t", n2)
        n3_t = load_list("n3_t", n3)
        n4_t = load_list("n4_t", n4)
        n5_t = load_list("n5_t", n5)

        g_rows = early.tile([P, P], F32, name="g_rows", align_bytes=64, offset=7 * 4096 - 256)
        nc.gpsimd.memset(g_rows[:], 0.0)
        for i, factor in enumerate((ga, gb)):
            nc.gpsimd.dma_start(
                g_rows[SLOTS * i : SLOTS * (i + 1), :].rearrange("t (b q) -> t b q", q=8),
                factor.rearrange("(b t q) o -> t b (q o)", t=SLOTS, q=8),
            )
        ws = early.tile([P, 2 * H], U8, name="ws", align_bytes=64, offset=3 * 4096 - 512)
        nc.vector.memset(ws[:].bitcast(I32), 0)
        ident = tile("ident", [P, P], F32)
        make_identity(nc, ident[:])
        a_win = [tile("a_win%d" % t, [P, 2 * S], F32) for t in range(SLOTS)]
        for t in range(SLOTS):
            nc.vector.memset(a_win[t][:, S:], 0.0)
        warm = tile("warm", [P, 1], F32)
        nc.scalar.activation(warm[:], a_win[0][:, S : S + 1], ACT.Exp)

        g_ps = bank(7, "g_ps", [P, P])
        nc.tensor.transpose(g_ps[:], g_rows[:], ident[:])
        ga_c = tile("ga_c", [P, SLOTS], F32)
        gb2_c = tile("gb2_c", [P, SLOTS], F32)
        nc.scalar.copy(ga_c[:], g_ps[:, 0:SLOTS])
        nc.scalar.activation(gb2_c[:], g_ps[:, SLOTS : 2 * SLOTS], ACT.Copy, scale=2.0)

        w_dealt = [early.tile([P, 2 * H], U8, name="w_dealt%d" % i, align_bytes=64, offset=7 * 4096 - 1024 * (1 - i)) for i in range(2)]
        nc.vector.tensor_copy(
            ws[0:16, :].bitcast(I32).rearrange("p (i t b w) -> p i t b w", i=2, t=SLOTS, w=2),
            ws_raw[:].bitcast(I32).rearrange("p (i b t w) -> p i t b w", i=2, t=SLOTS, w=2),
        )
        for q in range(1, 4):
            nc.scalar.dma_start(ws[32 * q : 32 * q + 4, :].bitcast(I32), ws[4 * q : 4 * q + 4, :].bitcast(I32))

        gs = [tile("gs0", [P, S], U8), early.tile([P, S], U8, name="gs1", align_bytes=64, offset=4096 - 256)]
        xsc = [tile("xsc%d" % i, [P, S], U8) for i in range(2)]
        for i, lst in enumerate((offs_t, two_t)):
            nc.vector.tensor_copy(gs[i][:], xs[:].indirect(lst[:]))
            nc.vector.tensor_copy(xsc[i][:].bitcast(I32), gs[i][:].bitcast(I32))
            for e in range(2):
                nc.scalar.dma_start(xsc[i][2 + e : P : 32, :].bitcast(I32), gs[i][16 + e : P : 32, :].bitcast(I32))
        gw = [early.tile([P, S], U32, name="gw%d" % i, align_bytes=64, offset=5 * 4096 - 1024 + 2048 * i) for i in range(2)]
        for i, lst in enumerate((offs_t, two_t)):
            nc.vector.tensor_copy(
                w_dealt[i][:].bitcast(I32).rearrange("p (t b w) -> p t b w", t=SLOTS, w=4),
                w_raw[i][:].bitcast(I32).rearrange("p (b t w) -> p t b w", t=SLOTS, w=4),
            )
            nc.vector.tensor_copy(gw[i][:], xw[:].bitcast(U32).indirect(lst[:]))

        def first_product(i, t, name):
            acc = bank(SLOTS * i + t, name, [P, S])
            nc.tensor.matmul_mx(
                acc[:],
                lhsT=w_dealt[i][:, 2 * P * t : 2 * P * (t + 1)].bitcast(FP4X4),
                lhsT_scale=ws[:, i * H + P * t : i * H + P * (t + 1)],
                rhs=gw[i][:].bitcast(FP8X4),
                rhs_scale=xsc[i][:],
                start=True, stop=True,
            )
            return acc

        ex = [tile("ex%d" % t, [P, V], F32) for t in range(SLOTS)]
        for t in range(SLOTS):
            a_ps = first_product(0, t, "a_ps%d" % t)
            if t == 0:
                nc.vector.tensor_scalar(a_win[t][:, :S], a_ps[:], ga_c[:, t : t + 1], None, ALU.mult)
            else:
                nc.scalar.activation(a_win[t][:, :S], a_ps[:], ACT.Copy, scale=ga_c[:, t : t + 1])
            b_ps = first_product(1, t, "b_ps%d" % t)
            nc.scalar.activation(ex[t][:], b_ps[:], ACT.Exp, scale=0.5)

        old = [early.tile([P, U], F32, name="old%d" % t, align_bytes=64, offset=4096 * t) for t in range(SLOTS)]
        page = [early.tile([P, U], F32, name="page%d" % t, align_bytes=64, offset=4096 * (SLOTS + t)) for t in range(SLOTS)]
        mem_v = mem.rearrange("(p t) u -> p t u", t=SLOTS)
        out_v = out_0.rearrange("(p t) u -> p t u", t=SLOTS)
        for dst in (old, page):
            for t in range(SLOTS):
                nc.sync.dma_start(dst[t][:], mem_v[:, t, :])

        pa = tile("pa", [P, SLOTS, S], BF16)
        pb = tile("pb", [P, SLOTS, S], BF16)
        lo = tile("lo", [P, SLOTS, S], BF16)
        hi = tile("hi", [P, SLOTS, S], BF16)
        mid = tile("mid", [P, SLOTS, S], BF16)
        z_pl = tile("z_pl", [P, SLOTS, S], BF16)
        for h in range(2):
            pair = slice(2 * h, 2 * h + 2)
            for t in (2 * h, 2 * h + 1):
                gather(False, pa[:, t, :], a_win[t][:], n1_t[:])
                gather(False, pb[:, t, :], a_win[t][:], n2_t[:])
            nc.vector.tensor_tensor(hi[:, pair, :], pa[:, pair, :], pb[:, pair, :], ALU.max)
            nc.vector.tensor_tensor(lo[:, pair, :], pa[:, pair, :], pb[:, pair, :], ALU.min)
            for t in (2 * h, 2 * h + 1):
                nc.vector.tensor_tensor(mid[:, t, :], a_win[t][:, :S], hi[:, t, :], ALU.min)
            for t in (2 * h, 2 * h + 1):
                nc.vector.tensor_tensor(z_pl[:, t, :], lo[:, t, :], mid[:, t, :], ALU.max)
        z_il = [tile("z_il%d" % h, [P, SLOTS * S // 2], BF16) for h in range(2)]
        for h in range(2):
            nc.vector.tensor_copy(
                z_il[h][:].rearrange("p (t a i s) -> p a t i s", t=2, i=2, s=SLOTS),
                z_pl[:].rearrange("p s (a i t) -> p a t i s", t=SLOTS, i=2)[:, :, 2 * h : 2 * h + 2, :, :],
            )
        zq = tile("zq", [P, S], U32)
        zs = tile("zs", [P, S], U8)
        for h in range(2):
            cols = slice(h * S // 2, (h + 1) * S // 2)
            nc.vector.quantize_mx(zq[:, cols].bitcast(FP8X4), zs[:, cols], z_il[h][:])

        def root_of_denominators(c):
            cols = slice(c * VC // 16, (c + 1) * VC // 16)
            g3 = tile("g3_%d" % c, [P, SLOTS, VC], F32)
            g4 = tile("g4_%d" % c, [P, SLOTS, VC], F32)
            for t in range(SLOTS):
                gather(True, g3[:, t, :], ex[t][:], n3_t[:, cols])
                gather(True, g4[:, t, :], ex[t][:], n4_t[:, cols])
            roots = []
            for vb in range(2):
                den = bank(4 * c + vb, "den%d_%d" % (c, vb), [P, SLOTS, P])
                for t in range(SLOTS):
                    blk = slice(vb * P, (vb + 1) * P)
                    terms = (ex[t][:, c * VC + vb * P : c * VC + (vb + 1) * P], g3[:, t, blk], g4[:, t, blk])
                    for n, term in enumerate(terms):
                        nc.tensor.matmul(den[:, t, :], term, ident[:], start=(n == 0), stop=(n == 2), is_transpose=True)
                rt = tile("rt%d_%d" % (c, vb), [P, SLOTS, P], F32)
                nc.scalar.activation(rt[:], den[:], ACT.Abs_reciprocal_sqrt)
                roots.append(rt)
            return roots

        def turn_back(c, vb, src):
            r = bank(4 + 2 * c + vb, "r%d_%d" % (c, vb), [P, SLOTS, P])
            for t in range(SLOTS):
                nc.tensor.transpose(r[:, t, :], src[:, t, :], ident[:])
            return r

        def second_factor(c):
            roots = root_of_denominators(c)
            r_ps = []
            for vb in range(2):
                sq = tile("sq%d_%d" % (c, vb), [P, SLOTS, P], F32)
                nc.scalar.activation(sq[:], roots[vb][:], ACT.Square)
                r_ps.append(turn_back(c, vb, sq))
            u = tile("u%d" % c, [P, 2, SLOTS, P], F32)
            for t in range(SLOTS):
                nc.scalar.activation(
                    u[:, :, t, :], ex[t][:, c * VC : (c + 1) * VC].rearrange("p (b v) -> p b v", b=2), ACT.Copy, scale=gb2_c[:, t : t + 1]
                )
            z2_il = [tile("z2_il%d_%d" % (c, vb), [P, SLOTS * P], BF16) for vb in range(2)]
            for vb in range(2):
                nc.vector.tensor_tensor(
                    z2_il[vb][:].rearrange("p (a i s) -> p a s i", i=4, s=SLOTS),
                    r_ps[vb][:].rearrange("p s (a i) -> p a s i", i=4),
                    u[:, vb, :, :].rearrange("p s (a i) -> p a s i", i=4),
                    ALU.mult,
                )
            return z2_il

        z2q = [tile("z2q%d" % c, [P, VC], U32) for c in range(CHUNKS)]
        z2s = [tile("z2s%d" % c, [P, VC], U8) for c in range(CHUNKS)]

        def quantise_block(c, vb, z2_il):
            cols = slice(vb * P, (vb + 1) * P)
            nc.vector.quantize_mx(z2q[c][:, cols].bitcast(FP8X4), z2s[c][:, cols], z2_il[vb][:])

        y_pl = tile("y_pl", [P, SLOTS, U], BF16)

        def scores(c):
            banks = []
            for h in range(2):
                s_ps = bank(2 * c + h, "s%d_%d" % (c, h), [P, 2, VC])
                for tt in range(2):
                    t = 2 * h + tt
                    nc.tensor.matmul_mx(
                        s_ps[:, tt, :],
                        lhsT=zq[:, P * t : P * (t + 1)].bitcast(FP8X4),
                        lhsT_scale=zs[:, P * t : P * (t + 1)],
                        rhs=z2q[c][:].bitcast(FP8X4),
                        rhs_scale=z2s[c][:],
                        start=True, stop=True,
                    )
                banks.append(s_ps)
            return banks

        def halved_old(c, t0, t1, tag):
            cols = slice(c * VC // 16, (c + 1) * VC // 16)
            held = sb.tile([P, t1 - t0, VC], F32, name="held%d_%d" % (c, t0), tag=tag, align_bytes=64)
            for t in range(t0, t1):
                nc.scalar.activation(held[:, t - t0, :], old[t][:].indirect(n5_t[:, cols]), ACT.Copy, scale=0.5)
            return held

        def new_values(c, t0, t1, s_banks, held, tag):
            nw = sb.tile([P, t1 - t0, VC], F32, name="nw%d_%d" % (c, t0), tag=tag, align_bytes=64)
            nc.vector.scalar_tensor_tensor(
                nw[:], s_banks[t0 // 2][:, t0 % 2 : t0 % 2 + t1 - t0, :], 0.0625, held[:], ALU.mult, ALU.max
            )
            return nw

        def write_page(c, t0, t1, nw):
            cols = slice(c * VC // 16, (c + 1) * VC // 16)
            for t in range(t0, t1):
                nc.vector.tensor_copy(page[t][:].indirect(n5_t[:, cols]), nw[:, t - t0, :])
                if c == CHUNKS - 1:
                    nc.sync.dma_start(out_v[:, t, :], page[t][:])
                    if t < SLOTS - 1:
                        nc.scalar.copy(y_pl[:, t, :], page[t][:])
                    else:
                        for n in range(2):
                            nc.vector.tensor_copy(y_pl[:, t, n * UQ : (n + 1) * UQ], page[t][:, n * UQ : (n + 1) * UQ])
                        nc.scalar.copy(y_pl[:, t, U // 2 :], page[t][:, U // 2 :])

        z2_il = second_factor(0)
        for vb in range(2):
            quantise_block(0, vb, z2_il)
        s_0 = scores(0)
        nw_a = new_values(0, 0, 2, s_0, halved_old(0, 0, 2, "held0_0"), "nw0_0")
        nw_b = new_values(0, 2, 3, s_0, halved_old(0, 2, 3, "held0_2"), "nw0_2")
        write_page(0, 0, 2, nw_a)
        write_page(0, 2, 3, nw_b)
        z2_il = second_factor(1)
        quantise_block(1, 0, z2_il)
        nw_c = new_values(0, 3, 4, s_0, halved_old(0, 3, 4, "rt1_1"), "u1")
        quantise_block(1, 1, z2_il)
        s_1 = scores(1)
        write_page(0, 3, 4, nw_c)
        nw_a = new_values(1, 0, 2, s_1, halved_old(1, 0, 2, "sq1_0"), "nw1_0")
        nw_b = new_values(1, 2, 4, s_1, halved_old(1, 2, 4, "sq1_1"), "nw1_2")
        write_page(1, 0, 2, nw_a)
        write_page(1, 2, 4, nw_b)

        ys = tile("ys", [P, U], U8)
        words_v = out_1[0].rearrange("p n t -> p (n t)").bitcast(I32)
        y_il = [tile("y_il%d" % n, [P, UQ, SLOTS], BF16) for n in range(QUARTERS)]
        for n in range(QUARTERS):
            dst = y_il[n][:].rearrange("p (a i) s -> p a s i", i=4)
            src = y_pl[:, :, n * UQ : (n + 1) * UQ].rearrange("p s (a i) -> p a s i", i=4)
            if n < 2:
                nc.vector.tensor_copy(dst, src)
            else:
                nc.scalar.copy(dst, src)
        for n0, n1q in ((0, 2), (2, 3), (3, 4)):
            yq = tile("yq%d" % n0, [P, (n1q - n0) * UQ], U32)
            for n in range(n0, n1q):
                nc.vector.quantize_mx(
                    yq[:, (n - n0) * UQ : (n - n0 + 1) * UQ].bitcast(FP8X4), ys[:, n * UQ : (n + 1) * UQ], y_il[n][:].rearrange("p v s -> p (v s)")
                )
            nc.sync.dma_start(words_v[:, n0 * UQ : n1q * UQ], yq[:].bitcast(I32))
        for q in range(4):
            queue = nc.sync if q < 2 else nc.scalar
            queue.dma_start(out_2[0, 4 * q : 4 * q + 4, :].bitcast(I32), ys[32 * q : 32 * q + 4, :].bitcast(I32))
